import numpy as np
import ml_dtypes


def mxq(x, axis, fmt="e4m3"):
    dtype, down = {"e4m3": (ml_dtypes.float8_e4m3fn, 7), "e5m2": (ml_dtypes.float8_e5m2, 14)}[fmt]
    v = np.moveaxis(np.asarray(x, np.float32).astype(ml_dtypes.bfloat16).astype(np.float64), axis, -1)
    blocks = v.reshape(v.shape[:-1] + (-1, 32))
    amax = np.abs(blocks).max(-1, keepdims=True)
    byte = np.maximum(np.where(amax > 0, np.frexp(amax)[1] - 1 + 127, 0) - down, 1)
    scale = np.exp2(byte - 127.0)
    codes = (blocks / scale).astype(np.float32).astype(dtype).astype(np.float64)
    return np.moveaxis((codes * scale).reshape(v.shape), -1, axis)


WIDE = False


def mx_kscale(k):
    if not WIDE:
        return np.ones(k)
    levels = np.array([10, -10, 5, -5, 0])
    if k % 512:
        return np.exp2(np.random.permutation(np.resize(levels, k // 32))).repeat(32)
    a = np.empty((k // 512, 16))
    for p in range(k // 512):
        a[p, :8] = np.random.permutation(np.resize(levels, 8))
        for g in range(8):
            far = levels[np.abs(levels - a[p, g]) >= 10]
            a[p, g + 8] = far[np.random.randint(len(far))]
    return np.exp2(a.ravel()).repeat(32)


def f64(x):
    return np.asarray(x).astype(np.float64)


def striped(idx):
    return np.tile(idx.reshape(-1, 16).T, (8, 1)).astype(np.uint16)


def unstriped(offs):
    return offs[:16].T.reshape(-1).astype(np.int64)


E2M1 = np.array([0.0, 0.5, 1.0, 1.5, 2.0, 3.0, 4.0, 6.0, -0.0, -0.5, -1.0, -1.5, -2.0, -3.0, -4.0, -6.0])


def pack_weight(w, fmt):
    k, n = w.shape
    w = f64(np.asarray(w, np.float32).astype(ml_dtypes.bfloat16)).reshape(k // 32, 32, n)
    amax = np.abs(w).max(1)
    if fmt == "e4m3":
        byte = np.frexp(amax)[1] - 1 + 127 - 7
    else:
        mant, ex = np.frexp(amax / 6.0)
        byte = np.where(mant > 0.5, ex, ex - 1) + 127
    byte = np.clip(np.where(amax > 0, byte, 1), 1, 254)
    scaled = (w * np.exp2(127.0 - byte)[:, None, :]).reshape(k, n).astype(np.float32)
    by_word = np.ascontiguousarray(scaled.reshape(k // 512, 128, 4, n).transpose(0, 1, 3, 2))
    if fmt == "e4m3":
        words = by_word.astype(ml_dtypes.float8_e4m3fn).view(np.uint8)
    else:
        c = by_word.astype(ml_dtypes.float4_e2m1fn).view(np.uint8) & 0xF
        words = (c[..., 0::2] | (c[..., 1::2] << 4)).reshape(k // 512, 128, 2 * n)
    return np.ascontiguousarray(words), np.ascontiguousarray(byte.astype(np.uint8).reshape(k // 512, 16, n))


def unpack_weight(words, scales, fmt):
    g, _, n = scales.shape
    words = np.ascontiguousarray(words).reshape(g, 128, n, -1)
    if fmt == "e4m3":
        vals = words.view(ml_dtypes.float8_e4m3fn).astype(np.float64)
    else:
        nib = np.empty((g, 128, n, 4), np.uint8)
        nib[..., 0::2] = words & 0xF
        nib[..., 1::2] = words >> 4
        vals = E2M1[nib]
    vals = vals * np.repeat(np.exp2(scales.astype(np.float64) - 127.0), 8, axis=1)[..., None]
    return vals.transpose(0, 1, 3, 2).reshape(g * 512, n)


def gelu(v):
    return 0.5 * v * (1.0 + np.tanh(np.sqrt(2.0 / np.pi) * (v + 0.044715 * v**3)))


K, T, S, H, T2, P, N = 1536, 2048, 1024, 512, 2048, 1024, 384

def setup_inputs():
    n = np.random.standard_normal
    s, u = mx_kscale(K)[:, None], mx_kscale(H)[:, None]
    d = {}
    d["tab_words"], d["tab_scales"] = pack_weight(n((K, T)) * s, "e4m3")
    d["offs"] = striped(np.random.permutation(T)[:S])
    d["w1"] = (1.5 * n((K, H)) / K**0.5 / s).astype(np.float32)
    d["gain"] = (1.4 * np.exp(0.3 * n(H)) * u[:, 0]).astype(np.float32)
    d["page0"] = (n((H, T2)) * u).astype(np.float32)
    d["wgs"] = np.exp(0.3 * n((128, S))).astype(np.float32)
    d["offs2"] = striped(np.random.permutation(T2)[:S])
    d["offs3"] = striped(np.random.permutation(T2)[:P])
    d["bx"] = (0.6 * n(H) * u[:, 0]).astype(np.float32)
    d["w2_words"], d["w2_scales"] = pack_weight(1.6 * n((H, N)) / H**0.5 / u, "e2m1")
    d["w3"] = (1.3 * n((H, N)) / H**0.5 / u).astype(np.float32)
    d["page1"] = n((N, T2)).astype(np.float32)
    d["wgo"] = np.exp(0.3 * n((128, P))).astype(np.float32)
    d["offs4"] = striped(np.random.permutation(T2)[:P])
    return d

def reference(tab_words, tab_scales, offs, w1, gain, page0, wgs, offs2, offs3, bx, w2_words, w2_scales, w3, page1, wgo, offs4):
    v = unpack_weight(tab_words, tab_scales, "e4m3")[:, unstriped(offs)]
    g1 = mxq(f64(w1), 0, "e4m3").T @ v
    h = f64(gain)[:, None] * (g1 / (1.0 + np.exp(-g1)))
    page = f64(page0).copy()
    page[:, unstriped(offs2)] = np.tile(f64(wgs), (H // 128, 1)) * h
    x = page[:, unstriped(offs3)] + f64(bx)[:, None]
    top = unpack_weight(w2_words, w2_scales, "e2m1").T @ mxq(x, 0, "e4m3")
    low = mxq(f64(w3), 0, "e4m3").T @ mxq(h, 0, "e4m3")
    y = top / (1.0 + np.abs(low))
    out = f64(page1).copy()
    out[:, unstriped(offs4)] = np.tile(f64(wgo), (N // 128, 1)) * y
    return out

@@ -1,0 +1,251 @@
+from contextlib import ExitStack
+
+import concourse.mybir as mybir
+
+K, T, S, H, T2, N = 1536, 2048, 1024, 512, 2048, 384
+FLOPS = 2 * K * H * S + 2 * 2 * H * N * S
+
+F32 = mybir.dt.float32
+BF16 = mybir.dt.bfloat16
+I32 = mybir.dt.int32
+U32 = mybir.dt.uint32
+U16 = mybir.dt.uint16
+U8 = mybir.dt.uint8
+FP8X4 = mybir.dt.float8_e4m3fn_x4
+FP4X4 = mybir.dt.float4_e2m1fn_x4
+ACT = mybir.ActivationFunctionType
+MULT = mybir.AluOpType.mult
+
+P = 128
+PACK = 4
+PASSES = K // (P * PACK)
+HALF = 512
+N_TILES = N // P
+CHUNKS = [(0, 256), (256, 512), (512, 1024)]
+
+
+def tile_list_rover_slip_page_kernel(
+    tc, tab_words, tab_scales, offs, w1, gain, page0, wgs, offs2, offs3, bx,
+    w2_words, w2_scales, w3, page1, wgo, offs4, out,
+):
+    nc = tc.nc
+    with ExitStack() as ctx:
+        keep = ctx.enter_context(tc.tile_pool(name="keep", bufs=1))
+        ring = ctx.enter_context(tc.tile_pool(name="ring", bufs=2))
+        psum = ctx.enter_context(tc.psum_pool(name="psum", bufs=1))
+
+        def held(shape, dtype, name, tag=None):
+            return keep.tile(shape, dtype, name=name, tag=tag or name, align_bytes=64)
+
+        def load_list(src, name):
+            tile = held([P, S // 16], U16, name)
+            nc.sync.dma_start(tile[:], src)
+            return tile
+
+        def entries(lst, lo, hi):
+            return lst[:, lo // 16 : hi // 16]
+
+        tab_sc = held([P, T], U8, "tab_sc")
+        nc.vector.memset(tab_sc[:].bitcast(I32), 0)
+        w2_sc = held([P, N], U8, "w2_sc")
+        nc.vector.memset(w2_sc[:].bitcast(I32), 0)
+
+        idx = load_list(offs, "idx")
+        w1_raw = [held([P, PACK, H], F32, f"w1_raw{a}") for a in range(PASSES)]
+        tab = [held([P, T], I32, f"tab{a}") for a in range(PASSES)]
+        for a in range(PASSES):
+            nc.sync.dma_start(w1_raw[a][:], w1[a * 512 : (a + 1) * 512, :].rearrange("(p j) c -> p j c", j=PACK))
+            if a == 0:
+                for q in range(4):
+                    nc.sync.dma_start(
+                        tab_sc[32 * q : 32 * q + 4 * PASSES, :].bitcast(I32),
+                        tab_scales[:, 4 * q : 4 * q + 4, :].bitcast(I32),
+                    )
+            nc.sync.dma_start(tab[a][:], tab_words[a].rearrange("p n t -> p (n t)").bitcast(I32))
+        gain_sb = held([P, PACK], F32, "gain_sb")
+        nc.sync.dma_start(gain_sb[:], gain.rearrange("(p t) -> p t", t=PACK))
+        idx2 = load_list(offs2, "idx2")
+
+        wgs_sb = {}
+        wgs_rows = wgs.rearrange("(m t) j -> m t j", t=PACK)
+        page0_rows = page0.rearrange("(p t) c -> p t c", t=PACK)
+        page = [held([P, T2], F32, f"page{t}") for t in range(PACK)]
+
+        def load_wgs(t, lo, hi):
+            tile = held([P, hi - lo], F32, f"wgs{t}_{lo}")
+            wgs_sb[(t, lo)] = tile
+            for q in range(4):
+                nc.sync.dma_start(tile[32 * q : 32 * q + 32, :], wgs_rows[:, t, lo:hi])
+
+        dest = [held([P, T2], F32, f"dest{c}") for c in range(N_TILES)]
+
+        def load_dest(c):
+            nc.sync.dma_start(dest[c][:], page1[c * P : (c + 1) * P, :])
+
+        def load_page(t):
+            nc.sync.dma_start(page[t][:], page0_rows[:, t, :])
+
+        load_wgs(0, 0, HALF)
+        load_page(0)
+        load_wgs(0, HALF, S)
+        load_wgs(1, 0, S)
+        load_page(1)
+        load_wgs(2, 0, S)
+        load_page(2)
+        w3_raw = held([P, PACK, N], F32, "w3_raw")
+        nc.sync.dma_start(w3_raw[:], w3.rearrange("(p j) c -> p j c", j=PACK))
+        wgo_sb = held([P, S], F32, "wgo_sb")
+        nc.sync.dma_start(wgo_sb[:], wgo)
+        load_dest(0)
+        idx3 = load_list(offs3, "idx3")
+        idx4 = load_list(offs4, "idx4")
+        bx_sb = held([P, PACK], F32, "bx_sb")
+        nc.sync.dma_start(bx_sb[:], bx.rearrange("(p t) -> p t", t=PACK))
+        w2_w = held([P, 2 * N], U8, "w2_w")
+        nc.sync.dma_start(w2_w[:].bitcast(I32), w2_words[0].bitcast(I32))
+        for q in range(4):
+            nc.sync.dma_start(
+                w2_sc[32 * q : 32 * q + 4, :].bitcast(I32), w2_scales[0, 4 * q : 4 * q + 4, :].bitcast(I32)
+            )
+        load_dest(1)
+        load_wgs(3, 0, S)
+        load_page(3)
+        load_dest(2)
+
+        v_sc = held([P, S], U8, "v_sc")
+        v_w = [held([P, S], U32, f"v_w{a}") for a in range(PASSES)]
+        w1_w = [held([P, H], U32, f"w1_w{a}") for a in range(PASSES)]
+        w1_sc = [held([P, H], U8, f"w1_sc{a}") for a in range(PASSES)]
+        for a in range(PASSES):
+            grouped = ring.tile([P, H * PACK], BF16, name="w1_bf", align_bytes=64)
+            dst = grouped[:].rearrange("p (t m j) -> p m t j", t=PACK, j=PACK)
+            src = w1_raw[a][:].rearrange("p j (m t) -> p m t j", t=PACK)
+            if a < PASSES - 1:
+                nc.scalar.copy(dst, src)
+            else:
+                nc.scalar.copy(dst[:, :64], src[:, :64])
+                nc.vector.tensor_copy(dst[:, 64:], src[:, 64:])
+            nc.vector.quantize_mx(out=w1_w[a][:].bitcast(FP8X4), scales=w1_sc[a][:], in_=grouped[:])
+            if a == 0:
+                nc.vector.tensor_copy(v_sc[:], tab_sc[:].indirect(idx[:]))
+            for lo in (0, HALF):
+                nc.vector.tensor_copy(
+                    v_w[a][:, lo : lo + HALF], tab[a][:].bitcast(U32).indirect(entries(idx, lo, lo + HALF))
+                )
+
+        def interleave(dst, src):
+            nc.scalar.copy(
+                dst.rearrange("p (c i t) -> p c t i", i=4, t=PACK),
+                src.rearrange("p t (c i) -> p c t i", i=4),
+            )
+
+        h = held([P, PACK, S], F32, "h", tag="hx")
+        w3_sc = held([P, N], U8, "w3_sc")
+        h_sc = held([P, S], U8, "h_sc")
+        damp = [held([P, S], F32, f"damp{c}") for c in range(N_TILES)]
+
+        def make_h(t, lo, bank):
+            acc = psum.tile([P, HALF], F32, name="acc", tag=f"bank{bank}")
+            for a in range(PASSES):
+                nc.tensor.matmul_mx(
+                    out=acc[:],
+                    lhsT=w1_w[a][:, t * P : (t + 1) * P].bitcast(FP8X4),
+                    lhsT_scale=w1_sc[a][:, t * P : (t + 1) * P],
+                    rhs=v_w[a][:, lo : lo + HALF].bitcast(FP8X4),
+                    rhs_scale=v_sc[4 * a : P, lo : lo + HALF],
+                    start=(a == 0),
+                    stop=(a == PASSES - 1),
+                )
+            part = h[:, t, lo : lo + HALF]
+            nc.scalar.activation(part, acc[:], ACT.Silu)
+            if (t, lo) == (0, 0):
+                nc.vector.tensor_scalar(part, part, gain_sb[:, t : t + 1], None, MULT)
+            else:
+                nc.scalar.activation(part, part, ACT.Copy, scale=gain_sb[:, t : t + 1])
+
+        def renew(t, lo, hi):
+            nc.vector.tensor_tensor(
+                page[t][:].indirect(entries(idx2, lo, hi)), h[:, t, lo:hi], wgs_sb[(t, lo)][:], MULT
+            )
+
+        for t in range(PACK):
+            make_h(t, 0, (2 * t) % 6)
+            make_h(t, HALF, (2 * t + 1) % 6)
+        h_bf = held([P, S * PACK], BF16, "h_bf")
+        interleave(h_bf[:], h[:])
+        w3_bf = held([P, N * PACK], BF16, "w3_bf")
+        interleave(w3_bf[:], w3_raw[:])
+        renew(0, 0, HALF)
+        renew(0, HALF, S)
+        renew(1, 0, S)
+        renew(2, 0, S)
+        h_w = held([P, S], U32, "h_w", tag="wgs2_0")
+        nc.vector.quantize_mx(out=h_w[:].bitcast(FP8X4), scales=h_sc[:], in_=h_bf[:])
+        w3_w = held([P, N], U32, "w3_w", tag="wgs1_0")
+        nc.vector.quantize_mx(out=w3_w[:].bitcast(FP8X4), scales=w3_sc[:], in_=w3_bf[:])
+        renew(PACK - 1, 0, S)
+
+        for c in range(N_TILES):
+            for lo in (0, HALF):
+                acc = psum.tile([P, HALF], F32, name="acc", tag=f"bank{2 * c + lo // HALF}")
+                nc.tensor.matmul_mx(
+                    out=acc[:],
+                    lhsT=w3_w[:, c * P : (c + 1) * P].bitcast(FP8X4),
+                    lhsT_scale=w3_sc[:, c * P : (c + 1) * P],
+                    rhs=h_w[:, lo : lo + HALF].bitcast(FP8X4),
+                    rhs_scale=h_sc[:, lo : lo + HALF],
+                    start=True,
+                    stop=True,
+                )
+                nc.scalar.activation(damp[c][:, lo : lo + HALF], acc[:], ACT.Abs)
+        for c in range(N_TILES):
+            nc.scalar.activation(damp[c][:], damp[c][:], ACT.Abs_reciprocal_sqrt, bias=1.0)
+        for c in range(N_TILES):
+            nc.scalar.activation(damp[c][:], damp[c][:], ACT.Square)
+
+        picked = held([P, PACK * S], F32, "picked", tag="hx")
+        x_w = held([P, S], U32, "x_w")
+        x_sc = held([P, S], U8, "x_sc")
+
+        def make_x(k):
+            lo, hi = CHUNKS[k]
+            n = hi - lo
+            x_rows = held([P, PACK, n], BF16, f"x_rows{k}")
+            for t in range(PACK):
+                if k == 2 and t == PACK - 1:
+                    got = held([P, n], F32, "last_pick", tag="x_bf0")[:]
+                else:
+                    got = picked[:, PACK * lo + t * n : PACK * lo + (t + 1) * n]
+                nc.vector.tensor_copy(got, page[t][:].indirect(entries(idx3, lo, hi)))
+                nc.scalar.activation(x_rows[:, t, :], got, ACT.Identity, bias=bx_sb[:, t : t + 1])
+            x_bf = held([P, n * PACK], BF16, f"x_bf{k}")
+            interleave(x_bf[:], x_rows[:])
+            nc.vector.quantize_mx(out=x_w[:, lo:hi].bitcast(FP8X4), scales=x_sc[:, lo:hi], in_=x_bf[:])
+
+        def place(k, c):
+            lo, hi = CHUNKS[k]
+            n = hi - lo
+            acc = psum.tile([P, n], F32, name="acc", tag=f"bank{4 + (N_TILES * k + c) % 4}")
+            nc.tensor.matmul_mx(
+                out=acc[:],
+                lhsT=w2_w[:, 2 * c * P : 2 * (c + 1) * P].bitcast(FP4X4),
+                lhsT_scale=w2_sc[:, c * P : (c + 1) * P],
+                rhs=x_w[:, lo:hi].bitcast(FP8X4),
+                rhs_scale=x_sc[:, lo:hi],
+                start=True,
+                stop=True,
+            )
+            if c == N_TILES - 1 and k + 1 < len(CHUNKS):
+                y = held([P, n], F32, f"y_last{k}", tag=f"x_bf{k + 1}")
+            else:
+                y = ring.tile([P, n], F32, name="y", align_bytes=64)
+            nc.vector.tensor_tensor(y[:], acc[:], damp[c][:, lo:hi], MULT)
+            nc.vector.tensor_tensor(dest[c][:].indirect(entries(idx4, lo, hi)), y[:], wgo_sb[:, lo:hi], MULT)
+
+        for k in range(len(CHUNKS)):
+            make_x(k)
+        for k in range(len(CHUNKS)):
+            for c in range(N_TILES):
+                place(k, c)
+        for c in range(N_TILES):
+            nc.sync.dma_start(out[c * P : (c + 1) * P, :], dest[c][:])

@@ -53,15 +53,23 @@ def tile_list_rover_slip_page_kernel(
         idx = load_list(offs, "idx")
         w1_raw = [held([P, PACK, H], F32, f"w1_raw{a}") for a in range(PASSES)]
         tab = [held([P, T], I32, f"tab{a}") for a in range(PASSES)]
-        for a in range(PASSES):
+
+        def load_w1(a):
             nc.sync.dma_start(w1_raw[a][:], w1[a * 512 : (a + 1) * 512, :].rearrange("(p j) c -> p j c", j=PACK))
-            if a == 0:
-                for q in range(4):
-                    nc.sync.dma_start(
-                        tab_sc[32 * q : 32 * q + 4 * PASSES, :].bitcast(I32),
-                        tab_scales[:, 4 * q : 4 * q + 4, :].bitcast(I32),
-                    )
+
+        def load_tab(a):
             nc.sync.dma_start(tab[a][:], tab_words[a].rearrange("p n t -> p (n t)").bitcast(I32))
+
+        load_tab(0)
+        load_w1(0)
+        for q in range(4):
+            nc.sync.dma_start(
+                tab_sc[32 * q : 32 * q + 4 * PASSES, :].bitcast(I32),
+                tab_scales[:, 4 * q : 4 * q + 4, :].bitcast(I32),
+            )
+        for a in range(1, PASSES):
+            load_w1(a)
+            load_tab(a)
         gain_sb = held([P, PACK], F32, "gain_sb")
         nc.sync.dma_start(gain_sb[:], gain.rearrange("(p t) -> p t", t=PACK))
         idx2 = load_list(offs2, "idx2")
@@ -74,7 +82,7 @@ def tile_list_rover_slip_page_kernel(
         def load_wgs(t, lo, hi):
             tile = held([P, hi - lo], F32, f"wgs{t}_{lo}")
             wgs_sb[(t, lo)] = tile
-            for q in range(4):
+            for q in (0, 2, 1, 3):
                 nc.sync.dma_start(tile[32 * q : 32 * q + 32, :], wgs_rows[:, t, lo:hi])
 
         dest = [held([P, T2], F32, f"dest{c}") for c in range(N_TILES)]
@@ -85,12 +93,13 @@ def tile_list_rover_slip_page_kernel(
         def load_page(t):
             nc.sync.dma_start(page[t][:], page0_rows[:, t, :])
 
-        load_wgs(0, 0, HALF)
+        load_wgs(0, 0, 256)
         load_page(0)
-        load_wgs(0, HALF, S)
+        load_wgs(0, 256, S)
         load_wgs(1, 0, S)
         load_page(1)
-        load_wgs(2, 0, S)
+        load_wgs(2, 0, HALF)
+        load_wgs(2, HALF, S)
         load_page(2)
         w3_raw = held([P, PACK, N], F32, "w3_raw")
         nc.sync.dma_start(w3_raw[:], w3.rearrange("(p j) c -> p j c", j=PACK))
@@ -128,10 +137,8 @@ def tile_list_rover_slip_page_kernel(
             nc.vector.quantize_mx(out=w1_w[a][:].bitcast(FP8X4), scales=w1_sc[a][:], in_=grouped[:])
             if a == 0:
                 nc.vector.tensor_copy(v_sc[:], tab_sc[:].indirect(idx[:]))
-            for lo in (0, HALF):
-                nc.vector.tensor_copy(
-                    v_w[a][:, lo : lo + HALF], tab[a][:].bitcast(U32).indirect(entries(idx, lo, lo + HALF))
-                )
+            for lo, hi in CHUNKS if a == PASSES - 1 else [(0, HALF), (HALF, S)]:
+                nc.vector.tensor_copy(v_w[a][:, lo:hi], tab[a][:].bitcast(U32).indirect(entries(idx, lo, hi)))
 
         def interleave(dst, src):
             nc.scalar.copy(
@@ -144,46 +151,49 @@ def tile_list_rover_slip_page_kernel(
         h_sc = held([P, S], U8, "h_sc")
         damp = [held([P, S], F32, f"damp{c}") for c in range(N_TILES)]
 
-        def make_h(t, lo, bank):
-            acc = psum.tile([P, HALF], F32, name="acc", tag=f"bank{bank}")
+        def make_h(t, lo, hi, bank):
+            acc = psum.tile([P, hi - lo], F32, name="acc", tag=f"bank{bank}")
             for a in range(PASSES):
                 nc.tensor.matmul_mx(
                     out=acc[:],
                     lhsT=w1_w[a][:, t * P : (t + 1) * P].bitcast(FP8X4),
                     lhsT_scale=w1_sc[a][:, t * P : (t + 1) * P],
-                    rhs=v_w[a][:, lo : lo + HALF].bitcast(FP8X4),
-                    rhs_scale=v_sc[4 * a : P, lo : lo + HALF],
+                    rhs=v_w[a][:, lo:hi].bitcast(FP8X4),
+                    rhs_scale=v_sc[4 * a : P, lo:hi],
                     start=(a == 0),
                     stop=(a == PASSES - 1),
                 )
-            part = h[:, t, lo : lo + HALF]
+            part = h[:, t, lo:hi]
             nc.scalar.activation(part, acc[:], ACT.Silu)
-            if (t, lo) == (0, 0):
-                nc.vector.tensor_scalar(part, part, gain_sb[:, t : t + 1], None, MULT)
-            else:
-                nc.scalar.activation(part, part, ACT.Copy, scale=gain_sb[:, t : t + 1])
+            nc.scalar.activation(part, part, ACT.Copy, scale=gain_sb[:, t : t + 1])
 
-        def renew(t, lo, hi):
+        def renew(t, lo, hi, first):
             nc.vector.tensor_tensor(
-                page[t][:].indirect(entries(idx2, lo, hi)), h[:, t, lo:hi], wgs_sb[(t, lo)][:], MULT
+                page[t][:].indirect(entries(idx2, lo, hi)),
+                h[:, t, lo:hi],
+                wgs_sb[(t, first)][:, lo - first : hi - first],
+                MULT,
             )
 
-        for t in range(PACK):
-            make_h(t, 0, (2 * t) % 6)
-            make_h(t, HALF, (2 * t + 1) % 6)
+        pieces = [(0, lo, hi) for lo, hi in CHUNKS]
+        pieces = pieces + [(t, lo, lo + HALF) for t in range(1, PACK) for lo in (0, HALF)]
+        for number, (t, lo, hi) in enumerate(pieces):
+            make_h(t, lo, hi, number % 6)
         h_bf = held([P, S * PACK], BF16, "h_bf")
         interleave(h_bf[:], h[:])
         w3_bf = held([P, N * PACK], BF16, "w3_bf")
         interleave(w3_bf[:], w3_raw[:])
-        renew(0, 0, HALF)
-        renew(0, HALF, S)
-        renew(1, 0, S)
-        renew(2, 0, S)
+        renew(0, 0, 256, 0)
+        renew(0, 256, HALF, 256)
+        renew(0, HALF, S, 256)
+        renew(1, 0, S, 0)
+        renew(2, 0, HALF, 0)
         h_w = held([P, S], U32, "h_w", tag="wgs2_0")
         nc.vector.quantize_mx(out=h_w[:].bitcast(FP8X4), scales=h_sc[:], in_=h_bf[:])
         w3_w = held([P, N], U32, "w3_w", tag="wgs1_0")
         nc.vector.quantize_mx(out=w3_w[:].bitcast(FP8X4), scales=w3_sc[:], in_=w3_bf[:])
-        renew(PACK - 1, 0, S)
+        renew(2, HALF, S, HALF)
+        renew(PACK - 1, 0, S, 0)
 
         for c in range(N_TILES):
             for lo in (0, HALF):

@@ -96,29 +96,29 @@ def tile_list_rover_slip_page_kernel(
         load_wgs(0, 0, 256)
         load_page(0)
         load_wgs(0, 256, S)
-        load_wgs(1, 0, S)
         load_page(1)
-        load_wgs(2, 0, HALF)
-        load_wgs(2, HALF, S)
-        load_page(2)
+        load_wgs(1, 0, S)
         w3_raw = held([P, PACK, N], F32, "w3_raw")
         nc.sync.dma_start(w3_raw[:], w3.rearrange("(p j) c -> p j c", j=PACK))
+        load_wgs(2, 0, HALF)
+        load_page(2)
+        load_wgs(2, HALF, S)
+        load_page(3)
+        load_wgs(3, 0, S)
         wgo_sb = held([P, S], F32, "wgo_sb")
         nc.sync.dma_start(wgo_sb[:], wgo)
-        load_dest(0)
         idx3 = load_list(offs3, "idx3")
-        idx4 = load_list(offs4, "idx4")
         bx_sb = held([P, PACK], F32, "bx_sb")
         nc.sync.dma_start(bx_sb[:], bx.rearrange("(p t) -> p t", t=PACK))
         w2_w = held([P, 2 * N], U8, "w2_w")
         nc.sync.dma_start(w2_w[:].bitcast(I32), w2_words[0].bitcast(I32))
+        idx4 = load_list(offs4, "idx4")
+        load_dest(0)
         for q in range(4):
             nc.sync.dma_start(
                 w2_sc[32 * q : 32 * q + 4, :].bitcast(I32), w2_scales[0, 4 * q : 4 * q + 4, :].bitcast(I32)
             )
         load_dest(1)
-        load_wgs(3, 0, S)
-        load_page(3)
         load_dest(2)
 
         v_sc = held([P, S], U8, "v_sc")
@@ -188,10 +188,11 @@ def tile_list_rover_slip_page_kernel(
         renew(0, HALF, S, 256)
         renew(1, 0, S, 0)
         renew(2, 0, HALF, 0)
-        h_w = held([P, S], U32, "h_w", tag="wgs2_0")
-        nc.vector.quantize_mx(out=h_w[:].bitcast(FP8X4), scales=h_sc[:], in_=h_bf[:])
-        w3_w = held([P, N], U32, "w3_w", tag="wgs1_0")
-        nc.vector.quantize_mx(out=w3_w[:].bitcast(FP8X4), scales=w3_sc[:], in_=w3_bf[:])
+        codes = held([P, S + N], U32, "codes", tag="wgs2_0")
+        h_w = codes[:, :S]
+        w3_w = codes[:, S:]
+        nc.vector.quantize_mx(out=h_w.bitcast(FP8X4), scales=h_sc[:], in_=h_bf[:])
+        nc.vector.quantize_mx(out=w3_w.bitcast(FP8X4), scales=w3_sc[:], in_=w3_bf[:])
         renew(2, HALF, S, HALF)
         renew(PACK - 1, 0, S, 0)
 

@@ -93,32 +93,32 @@ def tile_list_rover_slip_page_kernel(
         def load_page(t):
             nc.sync.dma_start(page[t][:], page0_rows[:, t, :])
 
-        load_wgs(0, 0, 256)
+        load_wgs(0, 0, HALF)
         load_page(0)
-        load_wgs(0, 256, S)
+        load_wgs(0, HALF, S)
         load_page(1)
         load_wgs(1, 0, S)
         w3_raw = held([P, PACK, N], F32, "w3_raw")
         nc.sync.dma_start(w3_raw[:], w3.rearrange("(p j) c -> p j c", j=PACK))
-        load_wgs(2, 0, HALF)
         load_page(2)
-        load_wgs(2, HALF, S)
+        load_wgs(2, 0, HALF)
         load_page(3)
-        load_wgs(3, 0, S)
+        load_wgs(2, HALF, S)
         wgo_sb = held([P, S], F32, "wgo_sb")
         nc.sync.dma_start(wgo_sb[:], wgo)
+        load_wgs(3, 0, S)
+        load_dest(0)
         idx3 = load_list(offs3, "idx3")
         bx_sb = held([P, PACK], F32, "bx_sb")
         nc.sync.dma_start(bx_sb[:], bx.rearrange("(p t) -> p t", t=PACK))
         w2_w = held([P, 2 * N], U8, "w2_w")
         nc.sync.dma_start(w2_w[:].bitcast(I32), w2_words[0].bitcast(I32))
         idx4 = load_list(offs4, "idx4")
-        load_dest(0)
+        load_dest(1)
         for q in range(4):
             nc.sync.dma_start(
                 w2_sc[32 * q : 32 * q + 4, :].bitcast(I32), w2_scales[0, 4 * q : 4 * q + 4, :].bitcast(I32)
             )
-        load_dest(1)
         load_dest(2)
 
         v_sc = held([P, S], U8, "v_sc")
@@ -149,7 +149,7 @@ def tile_list_rover_slip_page_kernel(
         h = held([P, PACK, S], F32, "h", tag="hx")
         w3_sc = held([P, N], U8, "w3_sc")
         h_sc = held([P, S], U8, "h_sc")
-        damp = [held([P, S], F32, f"damp{c}") for c in range(N_TILES)]
+        damp = [held([P, S], F32, f"damp{c}", tag=f"w1_raw{c}") for c in range(N_TILES)]
 
         def make_h(t, lo, hi, bank):
             acc = psum.tile([P, hi - lo], F32, name="acc", tag=f"bank{bank}")
@@ -167,52 +167,62 @@ def tile_list_rover_slip_page_kernel(
             nc.scalar.activation(part, acc[:], ACT.Silu)
             nc.scalar.activation(part, part, ACT.Copy, scale=gain_sb[:, t : t + 1])
 
-        def renew(t, lo, hi, first):
+        def renew(t, lo, hi):
             nc.vector.tensor_tensor(
-                page[t][:].indirect(entries(idx2, lo, hi)),
-                h[:, t, lo:hi],
-                wgs_sb[(t, first)][:, lo - first : hi - first],
-                MULT,
+                page[t][:].indirect(entries(idx2, lo, hi)), h[:, t, lo:hi], wgs_sb[(t, lo)][:], MULT
             )
 
         pieces = [(0, lo, hi) for lo, hi in CHUNKS]
         pieces = pieces + [(t, lo, lo + HALF) for t in range(1, PACK) for lo in (0, HALF)]
         for number, (t, lo, hi) in enumerate(pieces):
             make_h(t, lo, hi, number % 6)
-        h_bf = held([P, S * PACK], BF16, "h_bf")
-        interleave(h_bf[:], h[:])
+        h_bf = [held([P, HALF * PACK], BF16, f"h_bf{u}") for u in range(2)]
         w3_bf = held([P, N * PACK], BF16, "w3_bf")
+        interleave(h_bf[0][:], h[:, :, :HALF])
         interleave(w3_bf[:], w3_raw[:])
-        renew(0, 0, 256, 0)
-        renew(0, 256, HALF, 256)
-        renew(0, HALF, S, 256)
-        renew(1, 0, S, 0)
-        renew(2, 0, HALF, 0)
-        codes = held([P, S + N], U32, "codes", tag="wgs2_0")
-        h_w = codes[:, :S]
-        w3_w = codes[:, S:]
-        nc.vector.quantize_mx(out=h_w.bitcast(FP8X4), scales=h_sc[:], in_=h_bf[:])
+        interleave(h_bf[1][:], h[:, :, HALF:])
+        renew(0, 0, HALF)
+        renew(0, HALF, S)
+        renew(1, 0, S)
+        renew(2, 0, HALF)
+        codes = held([P, HALF + N], U32, "codes", tag="wgs2_0")
+        w3_w = codes[:, HALF:]
+        nc.vector.quantize_mx(out=codes[:, :HALF].bitcast(FP8X4), scales=h_sc[:, :HALF], in_=h_bf[0][:])
         nc.vector.quantize_mx(out=w3_w.bitcast(FP8X4), scales=w3_sc[:], in_=w3_bf[:])
-        renew(2, HALF, S, HALF)
-        renew(PACK - 1, 0, S, 0)
+        renew(2, HALF, S)
+        codes_hi = held([P, HALF], U32, "codes_hi", tag="wgs2_512")
+        nc.vector.quantize_mx(out=codes_hi[:].bitcast(FP8X4), scales=h_sc[:, HALF:], in_=h_bf[1][:])
+        renew(3, 0, S)
+        h_w = [codes[:, :HALF], codes_hi[:]]
 
-        for c in range(N_TILES):
-            for lo in (0, HALF):
-                acc = psum.tile([P, HALF], F32, name="acc", tag=f"bank{2 * c + lo // HALF}")
+        for u in range(2):
+            lo, hi = u * HALF, (u + 1) * HALF
+            for c in range(N_TILES):
+                acc = psum.tile([P, HALF], F32, name="acc", tag=f"bank{N_TILES * u + c}")
                 nc.tensor.matmul_mx(
                     out=acc[:],
                     lhsT=w3_w[:, c * P : (c + 1) * P].bitcast(FP8X4),
                     lhsT_scale=w3_sc[:, c * P : (c + 1) * P],
-                    rhs=h_w[:, lo : lo + HALF].bitcast(FP8X4),
-                    rhs_scale=h_sc[:, lo : lo + HALF],
+                    rhs=h_w[u].bitcast(FP8X4),
+                    rhs_scale=h_sc[:, lo:hi],
                     start=True,
                     stop=True,
                 )
-                nc.scalar.activation(damp[c][:, lo : lo + HALF], acc[:], ACT.Abs)
-        for c in range(N_TILES):
-            nc.scalar.activation(damp[c][:], damp[c][:], ACT.Abs_reciprocal_sqrt, bias=1.0)
-        for c in range(N_TILES):
-            nc.scalar.activation(damp[c][:], damp[c][:], ACT.Square)
+                nc.scalar.activation(damp[c][:, lo:hi], acc[:], ACT.Abs)
+            for c in range(N_TILES):
+                nc.scalar.activation(damp[c][:, lo:hi], damp[c][:, lo:hi], ACT.Abs_reciprocal_sqrt, bias=1.0)
+            for c in range(N_TILES):
+                nc.scalar.activation(damp[c][:, lo:hi], damp[c][:, lo:hi], ACT.Square)
+
+        factor = held([P, N_TILES * S], F32, "factor", tag="wgs3_0")
+        for lo in (0, HALF):
+            for c in range(N_TILES):
+                nc.gpsimd.tensor_tensor(
+                    factor[:, c * S + lo : c * S + lo + HALF],
+                    damp[c][:, lo : lo + HALF],
+                    wgo_sb[:, lo : lo + HALF],
+                    MULT,
+                )
 
         picked = held([P, PACK * S], F32, "picked", tag="hx")
         x_w = held([P, S], U32, "x_w")
@@ -225,6 +235,8 @@ def tile_list_rover_slip_page_kernel(
             for t in range(PACK):
                 if k == 2 and t == PACK - 1:
                     got = held([P, n], F32, "last_pick", tag="x_bf0")[:]
+                elif k == 2 and t == PACK - 2:
+                    got = held([P, n], F32, "late_pick", tag="x_rows0")[:]
                 else:
                     got = picked[:, PACK * lo + t * n : PACK * lo + (t + 1) * n]
                 nc.vector.tensor_copy(got, page[t][:].indirect(entries(idx3, lo, hi)))
@@ -249,13 +261,16 @@ def tile_list_rover_slip_page_kernel(
             if c == N_TILES - 1 and k + 1 < len(CHUNKS):
                 y = held([P, n], F32, f"y_last{k}", tag=f"x_bf{k + 1}")
             else:
-                y = ring.tile([P, n], F32, name="y", align_bytes=64)
-            nc.vector.tensor_tensor(y[:], acc[:], damp[c][:, lo:hi], MULT)
-            nc.vector.tensor_tensor(dest[c][:].indirect(entries(idx4, lo, hi)), y[:], wgo_sb[:, lo:hi], MULT)
+                y = ring.tile([P, n], F32, name="y", bufs=4, align_bytes=64)
+            nc.scalar.copy(y[:], acc[:])
+            nc.vector.tensor_tensor(
+                dest[c][:].indirect(entries(idx4, lo, hi)), y[:], factor[:, c * S + lo : c * S + hi], MULT
+            )
 
+        make_x(0)
         for k in range(len(CHUNKS)):
-            make_x(k)
-        for k in range(len(CHUNKS)):
+            if k + 1 < len(CHUNKS):
+                make_x(k + 1)
             for c in range(N_TILES):
                 place(k, c)
         for c in range(N_TILES):

@@ -18,10 +18,15 @@ MULT = mybir.AluOpType.mult
 
 P = 128
 PACK = 4
-PASSES = K // (P * PACK)
-HALF = 512
+K_PASS = P * PACK
+PASSES = K // K_PASS
+QUARTER = 32
+HALF = S // 2
+HALVES = [(0, HALF), (HALF, S)]
 N_TILES = N // P
-CHUNKS = [(0, 256), (256, 512), (512, 1024)]
+CHUNKS = [(0, HALF // 2), (HALF // 2, HALF), (HALF, S)]
+H_BANKS = 6
+TOP_BANKS = [4, 5, 6, 7]
 
 
 def tile_list_rover_slip_page_kernel(
@@ -45,6 +50,12 @@ def tile_list_rover_slip_page_kernel(
         def entries(lst, lo, hi):
             return lst[:, lo // 16 : hi // 16]
 
+        def interleave(dst, src):
+            nc.scalar.copy(
+                dst.rearrange("p (c i t) -> p c t i", i=4, t=PACK),
+                src.rearrange("p t (c i) -> p c t i", i=4),
+            )
+
         tab_sc = held([P, T], U8, "tab_sc")
         nc.vector.memset(tab_sc[:].bitcast(I32), 0)
         w2_sc = held([P, N], U8, "w2_sc")
@@ -55,7 +66,8 @@ def tile_list_rover_slip_page_kernel(
         tab = [held([P, T], I32, f"tab{a}") for a in range(PASSES)]
 
         def load_w1(a):
-            nc.sync.dma_start(w1_raw[a][:], w1[a * 512 : (a + 1) * 512, :].rearrange("(p j) c -> p j c", j=PACK))
+            rows = w1[a * K_PASS : (a + 1) * K_PASS, :]
+            nc.sync.dma_start(w1_raw[a][:], rows.rearrange("(p j) c -> p j c", j=PACK))
 
         def load_tab(a):
             nc.sync.dma_start(tab[a][:], tab_words[a].rearrange("p n t -> p (n t)").bitcast(I32))
@@ -64,7 +76,7 @@ def tile_list_rover_slip_page_kernel(
         load_w1(0)
         for q in range(4):
             nc.sync.dma_start(
-                tab_sc[32 * q : 32 * q + 4 * PASSES, :].bitcast(I32),
+                tab_sc[QUARTER * q : QUARTER * q + 4 * PASSES, :].bitcast(I32),
                 tab_scales[:, 4 * q : 4 * q + 4, :].bitcast(I32),
             )
         for a in range(1, PASSES):
@@ -83,7 +95,7 @@ def tile_list_rover_slip_page_kernel(
             tile = held([P, hi - lo], F32, f"wgs{t}_{lo}")
             wgs_sb[(t, lo)] = tile
             for q in (0, 2, 1, 3):
-                nc.sync.dma_start(tile[32 * q : 32 * q + 32, :], wgs_rows[:, t, lo:hi])
+                nc.sync.dma_start(tile[QUARTER * q : QUARTER * (q + 1), :], wgs_rows[:, t, lo:hi])
 
         dest = [held([P, T2], F32, f"dest{c}") for c in range(N_TILES)]
 
@@ -117,7 +129,8 @@ def tile_list_rover_slip_page_kernel(
         load_dest(1)
         for q in range(4):
             nc.sync.dma_start(
-                w2_sc[32 * q : 32 * q + 4, :].bitcast(I32), w2_scales[0, 4 * q : 4 * q + 4, :].bitcast(I32)
+                w2_sc[QUARTER * q : QUARTER * q + 4, :].bitcast(I32),
+                w2_scales[0, 4 * q : 4 * q + 4, :].bitcast(I32),
             )
         load_dest(2)
 
@@ -126,33 +139,27 @@ def tile_list_rover_slip_page_kernel(
         w1_w = [held([P, H], U32, f"w1_w{a}") for a in range(PASSES)]
         w1_sc = [held([P, H], U8, f"w1_sc{a}") for a in range(PASSES)]
         for a in range(PASSES):
-            grouped = ring.tile([P, H * PACK], BF16, name="w1_bf", align_bytes=64)
-            dst = grouped[:].rearrange("p (t m j) -> p m t j", t=PACK, j=PACK)
+            last_pass = a == PASSES - 1
+            w1_bf = ring.tile([P, H * PACK], BF16, name="w1_bf", align_bytes=64)
+            dst = w1_bf[:].rearrange("p (t m j) -> p m t j", t=PACK, j=PACK)
             src = w1_raw[a][:].rearrange("p j (m t) -> p m t j", t=PACK)
-            if a < PASSES - 1:
-                nc.scalar.copy(dst, src)
+            if last_pass:
+                nc.scalar.copy(dst[:, : P // 2], src[:, : P // 2])
+                nc.vector.tensor_copy(dst[:, P // 2 :], src[:, P // 2 :])
             else:
-                nc.scalar.copy(dst[:, :64], src[:, :64])
-                nc.vector.tensor_copy(dst[:, 64:], src[:, 64:])
-            nc.vector.quantize_mx(out=w1_w[a][:].bitcast(FP8X4), scales=w1_sc[a][:], in_=grouped[:])
+                nc.scalar.copy(dst, src)
+            nc.vector.quantize_mx(out=w1_w[a][:].bitcast(FP8X4), scales=w1_sc[a][:], in_=w1_bf[:])
             if a == 0:
                 nc.vector.tensor_copy(v_sc[:], tab_sc[:].indirect(idx[:]))
-            for lo, hi in CHUNKS if a == PASSES - 1 else [(0, HALF), (HALF, S)]:
+            for lo, hi in CHUNKS if last_pass else HALVES:
                 nc.vector.tensor_copy(v_w[a][:, lo:hi], tab[a][:].bitcast(U32).indirect(entries(idx, lo, hi)))
 
-        def interleave(dst, src):
-            nc.scalar.copy(
-                dst.rearrange("p (c i t) -> p c t i", i=4, t=PACK),
-                src.rearrange("p t (c i) -> p c t i", i=4),
-            )
-
-        h = held([P, PACK, S], F32, "h", tag="hx")
+        h = held([P, PACK, S], F32, "h")
         w3_sc = held([P, N], U8, "w3_sc")
         h_sc = held([P, S], U8, "h_sc")
-        damp = [held([P, S], F32, f"damp{c}", tag=f"w1_raw{c}") for c in range(N_TILES)]
-
-        def make_h(t, lo, hi, bank):
-            acc = psum.tile([P, hi - lo], F32, name="acc", tag=f"bank{bank}")
+        groups = [(0, lo, hi) for lo, hi in CHUNKS] + [(t, lo, hi) for t in range(1, PACK) for lo, hi in HALVES]
+        for number, (t, lo, hi) in enumerate(groups):
+            acc = psum.tile([P, hi - lo], F32, name="acc_h", tag=f"bank{number % H_BANKS}")
             for a in range(PASSES):
                 nc.tensor.matmul_mx(
                     out=acc[:],
@@ -163,42 +170,38 @@ def tile_list_rover_slip_page_kernel(
                     start=(a == 0),
                     stop=(a == PASSES - 1),
                 )
-            part = h[:, t, lo:hi]
-            nc.scalar.activation(part, acc[:], ACT.Silu)
-            nc.scalar.activation(part, part, ACT.Copy, scale=gain_sb[:, t : t + 1])
+            nc.scalar.activation(h[:, t, lo:hi], acc[:], ACT.Silu)
+            nc.scalar.activation(h[:, t, lo:hi], h[:, t, lo:hi], ACT.Copy, scale=gain_sb[:, t : t + 1])
+
+        h_bf = [held([P, HALF * PACK], BF16, f"h_bf{u}") for u in range(2)]
+        w3_bf = held([P, N * PACK], BF16, "w3_bf")
+        interleave(h_bf[0][:], h[:, :, :HALF])
+        interleave(w3_bf[:], w3_raw[:])
+        interleave(h_bf[1][:], h[:, :, HALF:])
 
         def renew(t, lo, hi):
             nc.vector.tensor_tensor(
                 page[t][:].indirect(entries(idx2, lo, hi)), h[:, t, lo:hi], wgs_sb[(t, lo)][:], MULT
             )
 
-        pieces = [(0, lo, hi) for lo, hi in CHUNKS]
-        pieces = pieces + [(t, lo, lo + HALF) for t in range(1, PACK) for lo in (0, HALF)]
-        for number, (t, lo, hi) in enumerate(pieces):
-            make_h(t, lo, hi, number % 6)
-        h_bf = [held([P, HALF * PACK], BF16, f"h_bf{u}") for u in range(2)]
-        w3_bf = held([P, N * PACK], BF16, "w3_bf")
-        interleave(h_bf[0][:], h[:, :, :HALF])
-        interleave(w3_bf[:], w3_raw[:])
-        interleave(h_bf[1][:], h[:, :, HALF:])
         renew(0, 0, HALF)
         renew(0, HALF, S)
         renew(1, 0, S)
         renew(2, 0, HALF)
-        codes = held([P, HALF + N], U32, "codes", tag="wgs2_0")
-        w3_w = codes[:, HALF:]
-        nc.vector.quantize_mx(out=codes[:, :HALF].bitcast(FP8X4), scales=h_sc[:, :HALF], in_=h_bf[0][:])
+        codes_first = held([P, HALF + N], U32, "codes_first", tag="wgs2_0")
+        w3_w = codes_first[:, HALF:]
+        nc.vector.quantize_mx(out=codes_first[:, :HALF].bitcast(FP8X4), scales=h_sc[:, :HALF], in_=h_bf[0][:])
         nc.vector.quantize_mx(out=w3_w.bitcast(FP8X4), scales=w3_sc[:], in_=w3_bf[:])
         renew(2, HALF, S)
-        codes_hi = held([P, HALF], U32, "codes_hi", tag="wgs2_512")
-        nc.vector.quantize_mx(out=codes_hi[:].bitcast(FP8X4), scales=h_sc[:, HALF:], in_=h_bf[1][:])
+        codes_second = held([P, HALF], U32, "codes_second", tag=f"wgs2_{HALF}")
+        nc.vector.quantize_mx(out=codes_second[:].bitcast(FP8X4), scales=h_sc[:, HALF:], in_=h_bf[1][:])
         renew(3, 0, S)
-        h_w = [codes[:, :HALF], codes_hi[:]]
+        h_w = [codes_first[:, :HALF], codes_second[:]]
 
-        for u in range(2):
-            lo, hi = u * HALF, (u + 1) * HALF
+        damp = [held([P, N_TILES, HALF], F32, f"damp{u}", tag=f"w1_raw{u}") for u in range(2)]
+        for u, (lo, hi) in enumerate(HALVES):
             for c in range(N_TILES):
-                acc = psum.tile([P, HALF], F32, name="acc", tag=f"bank{N_TILES * u + c}")
+                acc = psum.tile([P, HALF], F32, name="acc_low", tag=f"bank{N_TILES * u + c}")
                 nc.tensor.matmul_mx(
                     out=acc[:],
                     lhsT=w3_w[:, c * P : (c + 1) * P].bitcast(FP8X4),
@@ -208,35 +211,29 @@ def tile_list_rover_slip_page_kernel(
                     start=True,
                     stop=True,
                 )
-                nc.scalar.activation(damp[c][:, lo:hi], acc[:], ACT.Abs)
+                nc.scalar.activation(damp[u][:, c, :], acc[:], ACT.Abs)
             for c in range(N_TILES):
-                nc.scalar.activation(damp[c][:, lo:hi], damp[c][:, lo:hi], ACT.Abs_reciprocal_sqrt, bias=1.0)
+                nc.scalar.activation(damp[u][:, c, :], damp[u][:, c, :], ACT.Abs_reciprocal_sqrt, bias=1.0)
             for c in range(N_TILES):
-                nc.scalar.activation(damp[c][:, lo:hi], damp[c][:, lo:hi], ACT.Square)
+                nc.scalar.activation(damp[u][:, c, :], damp[u][:, c, :], ACT.Square)
 
-        factor = held([P, N_TILES * S], F32, "factor", tag="wgs3_0")
-        for lo in (0, HALF):
-            for c in range(N_TILES):
-                nc.gpsimd.tensor_tensor(
-                    factor[:, c * S + lo : c * S + lo + HALF],
-                    damp[c][:, lo : lo + HALF],
-                    wgo_sb[:, lo : lo + HALF],
-                    MULT,
-                )
+        factor = held([P, 2, N_TILES, HALF], F32, "factor", tag="wgs3_0")
+        for u, (lo, hi) in enumerate(HALVES):
+            wgo_all = wgo_sb[:, lo:hi].unsqueeze(1).to_broadcast([P, N_TILES, HALF])
+            nc.gpsimd.tensor_tensor(factor[:, u], damp[u][:], wgo_all, MULT)
 
-        picked = held([P, PACK * S], F32, "picked", tag="hx")
+        picked = held([P, PACK * S], F32, "picked", tag="h")
         x_w = held([P, S], U32, "x_w")
         x_sc = held([P, S], U8, "x_sc")
+        last_chunk = len(CHUNKS) - 1
 
         def make_x(k):
             lo, hi = CHUNKS[k]
             n = hi - lo
             x_rows = held([P, PACK, n], BF16, f"x_rows{k}")
             for t in range(PACK):
-                if k == 2 and t == PACK - 1:
+                if k == last_chunk and t == PACK - 1:
                     got = held([P, n], F32, "last_pick", tag="x_bf0")[:]
-                elif k == 2 and t == PACK - 2:
-                    got = held([P, n], F32, "late_pick", tag="x_rows0")[:]
                 else:
                     got = picked[:, PACK * lo + t * n : PACK * lo + (t + 1) * n]
                 nc.vector.tensor_copy(got, page[t][:].indirect(entries(idx3, lo, hi)))
@@ -248,7 +245,8 @@ def tile_list_rover_slip_page_kernel(
         def place(k, c):
             lo, hi = CHUNKS[k]
             n = hi - lo
-            acc = psum.tile([P, n], F32, name="acc", tag=f"bank{4 + (N_TILES * k + c) % 4}")
+            bank = TOP_BANKS[(N_TILES * k + c) % len(TOP_BANKS)]
+            acc = psum.tile([P, n], F32, name="acc_top", tag=f"bank{bank}")
             nc.tensor.matmul_mx(
                 out=acc[:],
                 lhsT=w2_w[:, 2 * c * P : 2 * (c + 1) * P].bitcast(FP4X4),
@@ -258,18 +256,22 @@ def tile_list_rover_slip_page_kernel(
                 start=True,
                 stop=True,
             )
-            if c == N_TILES - 1 and k + 1 < len(CHUNKS):
-                y = held([P, n], F32, f"y_last{k}", tag=f"x_bf{k + 1}")
+            if c == N_TILES - 1 and k < last_chunk:
+                top = held([P, n], F32, f"top_last{k}", tag=f"x_bf{k + 1}")
             else:
-                y = ring.tile([P, n], F32, name="y", bufs=4, align_bytes=64)
-            nc.scalar.copy(y[:], acc[:])
+                top = ring.tile([P, n], F32, name="top", bufs=4, align_bytes=64)
+            nc.scalar.copy(top[:], acc[:])
+            u = lo // HALF
             nc.vector.tensor_tensor(
-                dest[c][:].indirect(entries(idx4, lo, hi)), y[:], factor[:, c * S + lo : c * S + hi], MULT
+                dest[c][:].indirect(entries(idx4, lo, hi)),
+                top[:],
+                factor[:, u, c, lo - u * HALF : hi - u * HALF],
+                MULT,
             )
 
         make_x(0)
         for k in range(len(CHUNKS)):
-            if k + 1 < len(CHUNKS):
+            if k < last_chunk:
                 make_x(k + 1)
             for c in range(N_TILES):
                 place(k, c)

from contextlib import ExitStack

import concourse.mybir as mybir

K, T, S, H, T2, N = 1536, 2048, 1024, 512, 2048, 384
FLOPS = 2 * K * H * S + 2 * 2 * H * N * S

F32 = mybir.dt.float32
BF16 = mybir.dt.bfloat16
I32 = mybir.dt.int32
U32 = mybir.dt.uint32
U16 = mybir.dt.uint16
U8 = mybir.dt.uint8
FP8X4 = mybir.dt.float8_e4m3fn_x4
FP4X4 = mybir.dt.float4_e2m1fn_x4
ACT = mybir.ActivationFunctionType
MULT = mybir.AluOpType.mult

P = 128
PACK = 4
K_PASS = P * PACK
PASSES = K // K_PASS
QUARTER = 32
HALF = S // 2
HALVES = [(0, HALF), (HALF, S)]
N_TILES = N // P
CHUNKS = [(0, HALF // 2), (HALF // 2, HALF), (HALF, S)]
H_BANKS = 6
TOP_BANKS = [4, 5, 6, 7]


def tile_list_rover_slip_page_kernel(
    tc, tab_words, tab_scales, offs, w1, gain, page0, wgs, offs2, offs3, bx,
    w2_words, w2_scales, w3, page1, wgo, offs4, out,
):
    nc = tc.nc
    with ExitStack() as ctx:
        keep = ctx.enter_context(tc.tile_pool(name="keep", bufs=1))
        ring = ctx.enter_context(tc.tile_pool(name="ring", bufs=2))
        psum = ctx.enter_context(tc.psum_pool(name="psum", bufs=1))

        def held(shape, dtype, name, tag=None):
            return keep.tile(shape, dtype, name=name, tag=tag or name, align_bytes=64)

        def load_list(src, name):
            tile = held([P, S // 16], U16, name)
            nc.sync.dma_start(tile[:], src)
            return tile

        def entries(lst, lo, hi):
            return lst[:, lo // 16 : hi // 16]

        def interleave(dst, src):
            nc.scalar.copy(
                dst.rearrange("p (c i t) -> p c t i", i=4, t=PACK),
                src.rearrange("p t (c i) -> p c t i", i=4),
            )

        tab_sc = held([P, T], U8, "tab_sc")
        nc.vector.memset(tab_sc[:].bitcast(I32), 0)
        w2_sc = held([P, N], U8, "w2_sc")
        nc.vector.memset(w2_sc[:].bitcast(I32), 0)

        idx = load_list(offs, "idx")
        w1_raw = [held([P, PACK, H], F32, f"w1_raw{a}") for a in range(PASSES)]
        tab = [held([P, T], I32, f"tab{a}") for a in range(PASSES)]

        def load_w1(a):
            rows = w1[a * K_PASS : (a + 1) * K_PASS, :]
            nc.sync.dma_start(w1_raw[a][:], rows.rearrange("(p j) c -> p j c", j=PACK))

        def load_tab(a):
            nc.sync.dma_start(tab[a][:], tab_words[a].rearrange("p n t -> p (n t)").bitcast(I32))

        load_tab(0)
        load_w1(0)
        for q in range(4):
            nc.sync.dma_start(
                tab_sc[QUARTER * q : QUARTER * q + 4 * PASSES, :].bitcast(I32),
                tab_scales[:, 4 * q : 4 * q + 4, :].bitcast(I32),
            )
        for a in range(1, PASSES):
            load_w1(a)
            load_tab(a)
        gain_sb = held([P, PACK], F32, "gain_sb")
        nc.sync.dma_start(gain_sb[:], gain.rearrange("(p t) -> p t", t=PACK))
        idx2 = load_list(offs2, "idx2")

        wgs_sb = {}
        wgs_rows = wgs.rearrange("(m t) j -> m t j", t=PACK)
        page0_rows = page0.rearrange("(p t) c -> p t c", t=PACK)
        page = [held([P, T2], F32, f"page{t}") for t in range(PACK)]

        def load_wgs(t, lo, hi):
            tile = held([P, hi - lo], F32, f"wgs{t}_{lo}")
            wgs_sb[(t, lo)] = tile
            for q in (0, 2, 1, 3):
                nc.sync.dma_start(tile[QUARTER * q : QUARTER * (q + 1), :], wgs_rows[:, t, lo:hi])

        dest = [held([P, T2], F32, f"dest{c}") for c in range(N_TILES)]

        def load_dest(c):
            nc.sync.dma_start(dest[c][:], page1[c * P : (c + 1) * P, :])

        def load_page(t):
            nc.sync.dma_start(page[t][:], page0_rows[:, t, :])

        load_wgs(0, 0, HALF)
        load_page(0)
        load_wgs(0, HALF, S)
        load_page(1)
        load_wgs(1, 0, S)
        w3_raw = held([P, PACK, N], F32, "w3_raw")
        nc.sync.dma_start(w3_raw[:], w3.rearrange("(p j) c -> p j c", j=PACK))
        load_page(2)
        load_wgs(2, 0, HALF)
        load_page(3)
        load_wgs(2, HALF, S)
        wgo_sb = held([P, S], F32, "wgo_sb")
        nc.sync.dma_start(wgo_sb[:], wgo)
        load_wgs(3, 0, S)
        load_dest(0)
        idx3 = load_list(offs3, "idx3")
        bx_sb = held([P, PACK], F32, "bx_sb")
        nc.sync.dma_start(bx_sb[:], bx.rearrange("(p t) -> p t", t=PACK))
        w2_w = held([P, 2 * N], U8, "w2_w")
        nc.sync.dma_start(w2_w[:].bitcast(I32), w2_words[0].bitcast(I32))
        idx4 = load_list(offs4, "idx4")
        load_dest(1)
        for q in range(4):
            nc.sync.dma_start(
                w2_sc[QUARTER * q : QUARTER * q + 4, :].bitcast(I32),
                w2_scales[0, 4 * q : 4 * q + 4, :].bitcast(I32),
            )
        load_dest(2)

        v_sc = held([P, S], U8, "v_sc")
        v_w = [held([P, S], U32, f"v_w{a}") for a in range(PASSES)]
        w1_w = [held([P, H], U32, f"w1_w{a}") for a in range(PASSES)]
        w1_sc = [held([P, H], U8, f"w1_sc{a}") for a in range(PASSES)]
        for a in range(PASSES):
            last_pass = a == PASSES - 1
            w1_bf = ring.tile([P, H * PACK], BF16, name="w1_bf", align_bytes=64)
            dst = w1_bf[:].rearrange("p (t m j) -> p m t j", t=PACK, j=PACK)
            src = w1_raw[a][:].rearrange("p j (m t) -> p m t j", t=PACK)
            if last_pass:
                nc.scalar.copy(dst[:, : P // 2], src[:, : P // 2])
                nc.vector.tensor_copy(dst[:, P // 2 :], src[:, P // 2 :])
            else:
                nc.scalar.copy(dst, src)
            nc.vector.quantize_mx(out=w1_w[a][:].bitcast(FP8X4), scales=w1_sc[a][:], in_=w1_bf[:])
            if a == 0:
                nc.vector.tensor_copy(v_sc[:], tab_sc[:].indirect(idx[:]))
            for lo, hi in CHUNKS if last_pass else HALVES:
                nc.vector.tensor_copy(v_w[a][:, lo:hi], tab[a][:].bitcast(U32).indirect(entries(idx, lo, hi)))

        h = held([P, PACK, S], F32, "h")
        w3_sc = held([P, N], U8, "w3_sc")
        h_sc = held([P, S], U8, "h_sc")
        groups = [(0, lo, hi) for lo, hi in CHUNKS] + [(t, lo, hi) for t in range(1, PACK) for lo, hi in HALVES]
        for number, (t, lo, hi) in enumerate(groups):
            acc = psum.tile([P, hi - lo], F32, name="acc_h", tag=f"bank{number % H_BANKS}")
            for a in range(PASSES):
                nc.tensor.matmul_mx(
                    out=acc[:],
                    lhsT=w1_w[a][:, t * P : (t + 1) * P].bitcast(FP8X4),
                    lhsT_scale=w1_sc[a][:, t * P : (t + 1) * P],
                    rhs=v_w[a][:, lo:hi].bitcast(FP8X4),
                    rhs_scale=v_sc[4 * a : P, lo:hi],
                    start=(a == 0),
                    stop=(a == PASSES - 1),
                )
            nc.scalar.activation(h[:, t, lo:hi], acc[:], ACT.Silu)
            nc.scalar.activation(h[:, t, lo:hi], h[:, t, lo:hi], ACT.Copy, scale=gain_sb[:, t : t + 1])

        h_bf = [held([P, HALF * PACK], BF16, f"h_bf{u}") for u in range(2)]
        w3_bf = held([P, N * PACK], BF16, "w3_bf")
        interleave(h_bf[0][:], h[:, :, :HALF])
        interleave(w3_bf[:], w3_raw[:])
        interleave(h_bf[1][:], h[:, :, HALF:])

        def renew(t, lo, hi):
            nc.vector.tensor_tensor(
                page[t][:].indirect(entries(idx2, lo, hi)), h[:, t, lo:hi], wgs_sb[(t, lo)][:], MULT
            )

        renew(0, 0, HALF)
        renew(0, HALF, S)
        renew(1, 0, S)
        renew(2, 0, HALF)
        codes_first = held([P, HALF + N], U32, "codes_first", tag="wgs2_0")
        w3_w = codes_first[:, HALF:]
        nc.vector.quantize_mx(out=codes_first[:, :HALF].bitcast(FP8X4), scales=h_sc[:, :HALF], in_=h_bf[0][:])
        nc.vector.quantize_mx(out=w3_w.bitcast(FP8X4), scales=w3_sc[:], in_=w3_bf[:])
        renew(2, HALF, S)
        codes_second = held([P, HALF], U32, "codes_second", tag=f"wgs2_{HALF}")
        nc.vector.quantize_mx(out=codes_second[:].bitcast(FP8X4), scales=h_sc[:, HALF:], in_=h_bf[1][:])
        renew(3, 0, S)
        h_w = [codes_first[:, :HALF], codes_second[:]]

        damp = [held([P, N_TILES, HALF], F32, f"damp{u}", tag=f"w1_raw{u}") for u in range(2)]
        for u, (lo, hi) in enumerate(HALVES):
            for c in range(N_TILES):
                acc = psum.tile([P, HALF], F32, name="acc_low", tag=f"bank{N_TILES * u + c}")
                nc.tensor.matmul_mx(
                    out=acc[:],
                    lhsT=w3_w[:, c * P : (c + 1) * P].bitcast(FP8X4),
                    lhsT_scale=w3_sc[:, c * P : (c + 1) * P],
                    rhs=h_w[u].bitcast(FP8X4),
                    rhs_scale=h_sc[:, lo:hi],
                    start=True,
                    stop=True,
                )
                nc.scalar.activation(damp[u][:, c, :], acc[:], ACT.Abs)
            for c in range(N_TILES):
                nc.scalar.activation(damp[u][:, c, :], damp[u][:, c, :], ACT.Abs_reciprocal_sqrt, bias=1.0)
            for c in range(N_TILES):
                nc.scalar.activation(damp[u][:, c, :], damp[u][:, c, :], ACT.Square)

        factor = held([P, 2, N_TILES, HALF], F32, "factor", tag="wgs3_0")
        for u, (lo, hi) in enumerate(HALVES):
            wgo_all = wgo_sb[:, lo:hi].unsqueeze(1).to_broadcast([P, N_TILES, HALF])
            nc.gpsimd.tensor_tensor(factor[:, u], damp[u][:], wgo_all, MULT)

        picked = held([P, PACK * S], F32, "picked", tag="h")
        x_w = held([P, S], U32, "x_w")
        x_sc = held([P, S], U8, "x_sc")
        last_chunk = len(CHUNKS) - 1

        def make_x(k):
            lo, hi = CHUNKS[k]
            n = hi - lo
            x_rows = held([P, PACK, n], BF16, f"x_rows{k}")
            for t in range(PACK):
                if k == last_chunk and t == PACK - 1:
                    got = held([P, n], F32, "last_pick", tag="x_bf0")[:]
                else:
                    got = picked[:, PACK * lo + t * n : PACK * lo + (t + 1) * n]
                nc.vector.tensor_copy(got, page[t][:].indirect(entries(idx3, lo, hi)))
                nc.scalar.activation(x_rows[:, t, :], got, ACT.Identity, bias=bx_sb[:, t : t + 1])
            x_bf = held([P, n * PACK], BF16, f"x_bf{k}")
            interleave(x_bf[:], x_rows[:])
            nc.vector.quantize_mx(out=x_w[:, lo:hi].bitcast(FP8X4), scales=x_sc[:, lo:hi], in_=x_bf[:])

        def place(k, c):
            lo, hi = CHUNKS[k]
            n = hi - lo
            bank = TOP_BANKS[(N_TILES * k + c) % len(TOP_BANKS)]
            acc = psum.tile([P, n], F32, name="acc_top", tag=f"bank{bank}")
            nc.tensor.matmul_mx(
                out=acc[:],
                lhsT=w2_w[:, 2 * c * P : 2 * (c + 1) * P].bitcast(FP4X4),
                lhsT_scale=w2_sc[:, c * P : (c + 1) * P],
                rhs=x_w[:, lo:hi].bitcast(FP8X4),
                rhs_scale=x_sc[:, lo:hi],
                start=True,
                stop=True,
            )
            if c == N_TILES - 1 and k < last_chunk:
                top = held([P, n], F32, f"top_last{k}", tag=f"x_bf{k + 1}")
            else:
                top = ring.tile([P, n], F32, name="top", bufs=4, align_bytes=64)
            nc.scalar.copy(top[:], acc[:])
            u = lo // HALF
            nc.vector.tensor_tensor(
                dest[c][:].indirect(entries(idx4, lo, hi)),
                top[:],
                factor[:, u, c, lo - u * HALF : hi - u * HALF],
                MULT,
            )

        make_x(0)
        for k in range(len(CHUNKS)):
            if k < last_chunk:
                make_x(k + 1)
            for c in range(N_TILES):
                place(k, c)
        for c in range(N_TILES):
            nc.sync.dma_start(out[c * P : (c + 1) * P, :], dest[c][:])
